import numpy as np
import ml_dtypes


def mxq(x, axis, fmt="e4m3"):
    dtype, down = {"e4m3": (ml_dtypes.float8_e4m3fn, 7), "e5m2": (ml_dtypes.float8_e5m2, 14)}[fmt]
    v = np.moveaxis(np.asarray(x, np.float32).astype(ml_dtypes.bfloat16).astype(np.float64), axis, -1)
    blocks = v.reshape(v.shape[:-1] + (-1, 32))
    amax = np.abs(blocks).max(-1, keepdims=True)
    byte = np.maximum(np.where(amax > 0, np.frexp(amax)[1] - 1 + 127, 0) - down, 1)
    scale = np.exp2(byte - 127.0)
    codes = (blocks / scale).astype(np.float32).astype(dtype).astype(np.float64)
    return np.moveaxis((codes * scale).reshape(v.shape), -1, axis)


WIDE = False


def mx_kscale(k):
    if not WIDE:
        return np.ones(k)
    levels = np.array([10, -10, 5, -5, 0])
    if k % 512:
        return np.exp2(np.random.permutation(np.resize(levels, k // 32))).repeat(32)
    a = np.empty((k // 512, 16))
    for p in range(k // 512):
        a[p, :8] = np.random.permutation(np.resize(levels, 8))
        for g in range(8):
            far = levels[np.abs(levels - a[p, g]) >= 10]
            a[p, g + 8] = far[np.random.randint(len(far))]
    return np.exp2(a.ravel()).repeat(32)


def f64(x):
    return np.asarray(x).astype(np.float64)


def striped8(idx):
    return np.asarray(idx).reshape(8, -1, 16).transpose(0, 2, 1).reshape(128, -1).astype(np.uint16)


def unstriped8(offs):
    return offs.reshape(8, 16, -1).transpose(0, 2, 1).reshape(8, -1).astype(np.int64)


def pick8(x, idx, run):
    r = np.arange(len(x))
    return x[r[:, None], idx[r % (8 * run) // run]]


E2M1 = np.array([0.0, 0.5, 1.0, 1.5, 2.0, 3.0, 4.0, 6.0, -0.0, -0.5, -1.0, -1.5, -2.0, -3.0, -4.0, -6.0])


def pack_weight(w, fmt):
    k, n = w.shape
    w = f64(np.asarray(w, np.float32).astype(ml_dtypes.bfloat16)).reshape(k // 32, 32, n)
    amax = np.abs(w).max(1)
    if fmt == "e4m3":
        byte = np.frexp(amax)[1] - 1 + 127 - 7
    else:
        mant, ex = np.frexp(amax / 6.0)
        byte = np.where(mant > 0.5, ex, ex - 1) + 127
    byte = np.clip(np.where(amax > 0, byte, 1), 1, 254)
    scaled = (w * np.exp2(127.0 - byte)[:, None, :]).reshape(k, n).astype(np.float32)
    by_word = np.ascontiguousarray(scaled.reshape(k // 512, 128, 4, n).transpose(0, 1, 3, 2))
    if fmt == "e4m3":
        words = by_word.astype(ml_dtypes.float8_e4m3fn).view(np.uint8)
    else:
        c = by_word.astype(ml_dtypes.float4_e2m1fn).view(np.uint8) & 0xF
        words = (c[..., 0::2] | (c[..., 1::2] << 4)).reshape(k // 512, 128, 2 * n)
    return np.ascontiguousarray(words), np.ascontiguousarray(byte.astype(np.uint8).reshape(k // 512, 16, n))


def unpack_weight(words, scales, fmt):
    g, _, n = scales.shape
    words = np.ascontiguousarray(words).reshape(g, 128, n, -1)
    if fmt == "e4m3":
        vals = words.view(ml_dtypes.float8_e4m3fn).astype(np.float64)
    else:
        nib = np.empty((g, 128, n, 4), np.uint8)
        nib[..., 0::2] = words & 0xF
        nib[..., 1::2] = words >> 4
        vals = E2M1[nib]
    vals = vals * np.repeat(np.exp2(scales.astype(np.float64) - 127.0), 8, axis=1)[..., None]
    return vals.transpose(0, 1, 3, 2).reshape(g * 512, n)


D, T, U, X, S, I, Q = 512, 1024, 1024, 1024, 1024, 512, 128


def setup_inputs():
    n = np.random.standard_normal
    idx = np.stack([np.random.permutation(T)[:I] for _ in range(8)])
    idx2 = np.stack([np.random.permutation(U)[:I] for _ in range(8)])
    idx3 = np.stack([np.random.permutation(X)[:I] for _ in range(8)])
    idx4 = np.stack([np.random.permutation(X)[:I] for _ in range(8)])
    idx5 = np.stack([np.random.permutation(X)[:I] for _ in range(8)])
    idx6 = np.stack([np.random.permutation(S)[:I] for _ in range(8)])
    idx7 = np.stack([np.random.permutation(S)[:I] for _ in range(8)])
    fd = mx_kscale(D)
    keysp = pack_weight(n((D, T)) / fd[:, None], "e4m3")
    notesp = pack_weight(n((D, U)) / fd[:, None], "e2m1")
    usersp = pack_weight(n((D, X)) / fd[:, None], "e4m3")
    shelvesp = pack_weight(n((D, S)) / fd[:, None], "e2m1")
    return {
        "query": (n((D, Q)) * 1.0 / np.sqrt(D) * fd[:, None]).astype(np.float32),
        "keys_words": keysp[0],
        "keys_scales": keysp[1],
        "notes_words": notesp[0],
        "notes_scales": notesp[1],
        "users_words": usersp[0],
        "users_scales": usersp[1],
        "shelves_words": shelvesp[0],
        "shelves_scales": shelvesp[1],
        "offs": striped8(idx),
        "offs2": striped8(idx2),
        "offs3": striped8(idx3),
        "offs4": striped8(idx4),
        "offs5": striped8(idx5),
        "offs6": striped8(idx6),
        "offs7": striped8(idx7),
    }


def reference(query, keys_words, keys_scales, notes_words, notes_scales, users_words, users_scales, shelves_words, shelves_scales, offs, offs2, offs3, offs4, offs5, offs6, offs7):
    idx = unstriped8(offs)
    idx2 = unstriped8(offs2)
    idx3 = unstriped8(offs3)
    idx4 = unstriped8(offs4)
    idx5 = unstriped8(offs5)
    idx6 = unstriped8(offs6)
    idx7 = unstriped8(offs7)
    keysu = unpack_weight(keys_words, keys_scales, "e4m3")
    notesu = unpack_weight(notes_words, notes_scales, "e2m1")
    usersu = unpack_weight(users_words, users_scales, "e4m3")
    shelvesu = unpack_weight(shelves_words, shelves_scales, "e2m1")
    queryq = mxq(f64(query), 0, "e4m3")
    a = queryq.T @ keysu
    b = queryq.T @ notesu
    c0 = queryq.T @ usersu
    d0 = queryq.T @ shelvesu
    f1 = np.zeros((Q, X))
    f1[np.arange(Q)[:, None], idx3[np.arange(Q) % 128 // 16]] = pick8(a, idx, 16)
    f2 = np.zeros((Q, X))
    f2[np.arange(Q)[:, None], idx4[np.arange(Q) % 128 // 16]] = pick8(b, idx2, 16)
    m1 = np.minimum(f1, f2)
    cc = c0 + m1
    f3 = np.zeros((Q, S))
    f3[np.arange(Q)[:, None], idx6[np.arange(Q) % 128 // 16]] = pick8(cc, idx5, 16)
    dd = d0 - f3
    y = pick8(dd, idx7, 16)
    return y

@@ -1,0 +1,159 @@
+from contextlib import ExitStack
+
+import concourse.mybir as mybir
+
+D, COLS, SLOTS, Q = 512, 1024, 512, 128
+FLOPS = 4 * 2 * D * Q * COLS
+
+F32 = mybir.dt.float32
+BF16 = mybir.dt.bfloat16
+I32 = mybir.dt.int32
+U32 = mybir.dt.uint32
+U16 = mybir.dt.uint16
+U8 = mybir.dt.uint8
+FP8X4 = mybir.dt.float8_e4m3fn_x4
+FP4X4 = mybir.dt.float4_e2m1fn_x4
+ALU = mybir.AluOpType
+COPY = mybir.ActivationFunctionType.Copy
+
+P = 128
+PACK = 4
+BANK = 512
+HALF = SLOTS // 2
+LIST_COLS = SLOTS // 16
+
+
+def tile_attend_tributaries_four_kernel(
+    tc, query, keys_words, keys_scales, notes_words, notes_scales, users_words, users_scales,
+    shelves_words, shelves_scales, offs, offs2, offs3, offs4, offs5, offs6, offs7, out,
+):
+    nc = tc.nc
+    with ExitStack() as ctx:
+        lists = ctx.enter_context(tc.tile_pool(name="lists", bufs=1))
+        keep = ctx.enter_context(tc.tile_pool(name="keep", bufs=1))
+        psum = ctx.enter_context(tc.psum_pool(name="psum", bufs=1))
+
+        def load_list(name, source):
+            tile = lists.tile([P, LIST_COLS], U16, name=name)
+            nc.sync.dma_start(tile[:], source)
+            return tile
+
+        def load_scales(name, source):
+            plane = keep.tile([P, COLS], U8, name=name, align_bytes=64)
+            nc.vector.memset(plane[:].bitcast(I32), 0)
+            rows = source[0].bitcast(I32)
+            for r in range(4):
+                nc.sync.dma_start(plane[r:P:32, :].bitcast(I32), rows[r:16:4, :])
+            return plane
+
+        def load_words(name, source, bytes_per_column):
+            words = keep.tile([P, COLS * bytes_per_column], U8, name=name, align_bytes=64)
+            nc.sync.dma_start(words[:].bitcast(I32), source.bitcast(I32))
+            return words
+
+        def zeroed(name, tag):
+            tile = keep.tile([P, COLS], F32, name=name, tag=tag, align_bytes=64)
+            nc.vector.memset(tile[:].bitcast(I32), 0)
+            return tile
+
+        def first_half(tile):
+            return tile[:, 0 : LIST_COLS // 2]
+
+        def second_half(tile):
+            return tile[:, LIST_COLS // 2 : LIST_COLS]
+
+        def picked(name, window, offsets):
+            tile = keep.tile([P, SLOTS], F32, name=name)
+            nc.vector.tensor_copy(tile[:, 0:HALF], window[:].indirect(first_half(offsets)))
+            nc.scalar.activation(tile[:, HALF:SLOTS], window[:].indirect(second_half(offsets)), COPY)
+            return tile
+
+        q_raw = keep.tile([P, PACK, Q], F32, name="q_raw")
+        nc.sync.dma_start(q_raw[:], query.rearrange("(p j) w -> p j w", j=PACK))
+        notes_s = load_scales("notes_s", notes_scales)
+        notes_w = load_words("notes_w", notes_words[0], 2)
+        idx2 = load_list("idx2", offs2)
+        idx4 = load_list("idx4", offs4)
+        keys_s = load_scales("keys_s", keys_scales)
+        keys_w = load_words("keys_w", keys_words[0].rearrange("p n t -> p (n t)"), 4)
+        idx = load_list("idx", offs)
+        idx3 = load_list("idx3", offs3)
+        f2 = zeroed("f2", "f2")
+        f1 = zeroed("f1", "f1")
+        users_s = load_scales("users_s", users_scales)
+        users_w = load_words("users_w", users_words[0].rearrange("p n t -> p (n t)"), 4)
+        idx5 = load_list("idx5", offs5)
+        idx6 = load_list("idx6", offs6)
+        shelves_s = load_scales("shelves_s", shelves_scales)
+        shelves_w = load_words("shelves_w", shelves_words[0], 2)
+        idx7 = load_list("idx7", offs7)
+
+        q_grouped = keep.tile([P, Q, PACK], BF16, name="q_grouped", tag="late", align_bytes=64)
+        nc.scalar.activation(
+            q_grouped[:].rearrange("p (c i) t -> p c t i", i=4),
+            q_raw[:].rearrange("p t (c i) -> p c t i", i=4),
+            COPY,
+        )
+        q_codes = keep.tile([P, Q], U32, name="q_codes", align_bytes=64)
+        q_scales = keep.tile([P, Q], U8, name="q_scales", align_bytes=64)
+        nc.vector.quantize_mx(
+            out=q_codes[:].bitcast(FP8X4), scales=q_scales[:], in_=q_grouped[:].rearrange("p w j -> p (w j)")
+        )
+        f3 = zeroed("f3", "late")
+
+        def scores(name, bank, words, plane, dtype, bytes_per_column, start, width):
+            acc = psum.tile([P, width], F32, name=name, tag="bank%d" % bank)
+            nc.tensor.matmul_mx(
+                out=acc[:],
+                lhsT=q_codes[:].bitcast(FP8X4),
+                lhsT_scale=q_scales[:],
+                rhs=words[:, start * bytes_per_column : (start + width) * bytes_per_column].bitcast(dtype),
+                rhs_scale=plane[:, start : start + width],
+                start=True,
+                stop=True,
+            )
+            return acc
+
+        b = keep.tile([P, COLS], F32, name="b")
+        for piece in range(4):
+            acc = scores("b_acc%d" % piece, piece, notes_w, notes_s, FP4X4, 2, piece * 256, 256)
+            cols = slice(piece * 256, (piece + 1) * 256)
+            if piece % 2 == 0:
+                nc.scalar.activation(b[:, cols], acc[:], COPY)
+            else:
+                nc.vector.tensor_copy(b[:, cols], acc[:])
+        b_picked = picked("b_picked", b, idx2)
+        nc.vector.tensor_copy(f2[:].indirect(idx4[:]), b_picked[:])
+
+        a = keep.tile([P, COLS], F32, name="a")
+        for piece in range(2):
+            acc = scores("a_acc%d" % piece, 4 + piece, keys_w, keys_s, FP8X4, 4, piece * BANK, BANK)
+            nc.scalar.activation(a[:, piece * BANK : (piece + 1) * BANK], acc[:], COPY)
+        a_picked = keep.tile([P, SLOTS], F32, name="a_picked")
+        nc.scalar.activation(a_picked[:], a[:].indirect(idx[:]), COPY)
+        nc.vector.tensor_copy(f1[:].indirect(idx3[:]), a_picked[:])
+
+        c0 = [scores("c_acc%d" % h, 6 + h, users_w, users_s, FP8X4, 4, h * BANK, BANK) for h in range(2)]
+        d0 = [scores("d_acc%d" % h, h, shelves_w, shelves_s, FP4X4, 2, h * BANK, BANK) for h in range(2)]
+
+        m1 = keep.tile([P, COLS], F32, name="m1")
+        for h in range(2):
+            cols = slice(h * BANK, (h + 1) * BANK)
+            nc.vector.tensor_tensor(m1[:, cols], f1[:, cols], f2[:, cols], ALU.min)
+        cc = keep.tile([P, COLS], F32, name="cc")
+        for h in range(2):
+            cols = slice(h * BANK, (h + 1) * BANK)
+            nc.vector.tensor_tensor(cc[:, cols], c0[h][:], m1[:, cols], ALU.add)
+        cc_picked = picked("cc_picked", cc, idx5)
+        nc.vector.tensor_copy(f3[:].indirect(idx6[:]), cc_picked[:])
+
+        dd = keep.tile([P, COLS], F32, name="dd")
+        for h in range(2):
+            cols = slice(h * BANK, (h + 1) * BANK)
+            nc.vector.tensor_tensor(dd[:, cols], d0[h][:], f3[:, cols], ALU.subtract)
+        y_first = keep.tile([P, HALF], F32, name="y_first")
+        y_second = keep.tile([P, HALF], F32, name="y_second")
+        nc.vector.tensor_copy(y_first[:], dd[:].indirect(first_half(idx7)))
+        nc.scalar.activation(y_second[:], dd[:].indirect(second_half(idx7)), COPY)
+        nc.sync.dma_start(out[:, 0:HALF], y_first[:])
+        nc.scalar.dma_start(out[:, HALF:SLOTS], y_second[:])

@@ -38,13 +38,16 @@ def tile_attend_tributaries_four_kernel(
             nc.sync.dma_start(tile[:], source)
             return tile
 
-        def load_scales(name, source):
-            plane = keep.tile([P, COLS], U8, name=name, align_bytes=64)
-            nc.vector.memset(plane[:].bitcast(I32), 0)
+        def scale_tile(name, engine):
+            tile = keep.tile([P, COLS], U8, name=name, align_bytes=64)
+            engine.memset(tile[:].bitcast(I32), 0)
+            return tile
+
+        def load_scales(tile, first_row, source):
             rows = source[0].bitcast(I32)
             for r in range(4):
-                nc.sync.dma_start(plane[r:P:32, :].bitcast(I32), rows[r:16:4, :])
-            return plane
+                nc.sync.dma_start(tile[first_row + r : P : 32, :].bitcast(I32), rows[r:16:4, :])
+            return tile[first_row:P, :]
 
         def load_words(name, source, bytes_per_column):
             words = keep.tile([P, COLS * bytes_per_column], U8, name=name, align_bytes=64)
@@ -70,30 +73,30 @@ def tile_attend_tributaries_four_kernel(
 
         q_raw = keep.tile([P, PACK, Q], F32, name="q_raw")
         nc.sync.dma_start(q_raw[:], query.rearrange("(p j) w -> p j w", j=PACK))
-        notes_s = load_scales("notes_s", notes_scales)
+        notes_s = load_scales(scale_tile("notes_tile", nc.vector), 0, notes_scales)
         notes_w = load_words("notes_w", notes_words[0], 2)
         idx2 = load_list("idx2", offs2)
         idx4 = load_list("idx4", offs4)
-        keys_s = load_scales("keys_s", keys_scales)
         keys_w = load_words("keys_w", keys_words[0].rearrange("p n t -> p (n t)"), 4)
+        keys_s = load_scales(scale_tile("keys_tile", nc.gpsimd), 0, keys_scales)
         idx = load_list("idx", offs)
         idx3 = load_list("idx3", offs3)
         f2 = zeroed("f2", "f2")
         f1 = zeroed("f1", "f1")
-        users_s = load_scales("users_s", users_scales)
+        shared_tile = scale_tile("shared_tile", nc.gpsimd)
+        users_s = load_scales(shared_tile, 4, users_scales)
         users_w = load_words("users_w", users_words[0].rearrange("p n t -> p (n t)"), 4)
         idx5 = load_list("idx5", offs5)
         idx6 = load_list("idx6", offs6)
-        shelves_s = load_scales("shelves_s", shelves_scales)
+        shelves_s = load_scales(shared_tile, 0, shelves_scales)
         shelves_w = load_words("shelves_w", shelves_words[0], 2)
         idx7 = load_list("idx7", offs7)
 
         q_grouped = keep.tile([P, Q, PACK], BF16, name="q_grouped", tag="late", align_bytes=64)
-        nc.scalar.activation(
-            q_grouped[:].rearrange("p (c i) t -> p c t i", i=4),
-            q_raw[:].rearrange("p t (c i) -> p c t i", i=4),
-            COPY,
-        )
+        q_in = q_raw[:].rearrange("p t (c i) -> p c t i", i=4)
+        q_out = q_grouped[:].rearrange("p (c i) t -> p c t i", i=4)
+        nc.vector.tensor_copy(q_out[:, 0:16], q_in[:, 0:16])
+        nc.scalar.activation(q_out[:, 16:32], q_in[:, 16:32], COPY)
         q_codes = keep.tile([P, Q], U32, name="q_codes", align_bytes=64)
         q_scales = keep.tile([P, Q], U8, name="q_scales", align_bytes=64)
         nc.vector.quantize_mx(
@@ -115,9 +118,11 @@ def tile_attend_tributaries_four_kernel(
             return acc
 
         b = keep.tile([P, COLS], F32, name="b")
-        for piece in range(4):
-            acc = scores("b_acc%d" % piece, piece, notes_w, notes_s, FP4X4, 2, piece * 256, 256)
-            cols = slice(piece * 256, (piece + 1) * 256)
+        start = 0
+        for piece, width in enumerate((256, 256, 256, 128, 128)):
+            acc = scores("b_acc%d" % piece, piece, notes_w, notes_s, FP4X4, 2, start, width)
+            cols = slice(start, start + width)
+            start = start + width
             if piece % 2 == 0:
                 nc.scalar.activation(b[:, cols], acc[:], COPY)
             else:
@@ -127,14 +132,14 @@ def tile_attend_tributaries_four_kernel(
 
         a = keep.tile([P, COLS], F32, name="a")
         for piece in range(2):
-            acc = scores("a_acc%d" % piece, 4 + piece, keys_w, keys_s, FP8X4, 4, piece * BANK, BANK)
+            acc = scores("a_acc%d" % piece, 5 + piece, keys_w, keys_s, FP8X4, 4, piece * BANK, BANK)
             nc.scalar.activation(a[:, piece * BANK : (piece + 1) * BANK], acc[:], COPY)
         a_picked = keep.tile([P, SLOTS], F32, name="a_picked")
         nc.scalar.activation(a_picked[:], a[:].indirect(idx[:]), COPY)
         nc.vector.tensor_copy(f1[:].indirect(idx3[:]), a_picked[:])
 
-        c0 = [scores("c_acc%d" % h, 6 + h, users_w, users_s, FP8X4, 4, h * BANK, BANK) for h in range(2)]
-        d0 = [scores("d_acc%d" % h, h, shelves_w, shelves_s, FP4X4, 2, h * BANK, BANK) for h in range(2)]
+        c0 = [scores("c_acc%d" % h, h, users_w, users_s, FP8X4, 4, h * BANK, BANK) for h in range(2)]
+        d0 = [scores("d_acc%d" % h, 2 + h, shelves_w, shelves_s, FP4X4, 2, h * BANK, BANK) for h in range(2)]
 
         m1 = keep.tile([P, COLS], F32, name="m1")
         for h in range(2):

@@ -21,6 +21,8 @@ PACK = 4
 BANK = 512
 HALF = SLOTS // 2
 LIST_COLS = SLOTS // 16
+ADD_SHARE = 256
+SUBTRACT_SHARE = 304
 
 
 def tile_attend_tributaries_four_kernel(
@@ -69,6 +71,15 @@ def tile_attend_tributaries_four_kernel(
             tile = keep.tile([P, SLOTS], F32, name=name)
             nc.vector.tensor_copy(tile[:, 0:HALF], window[:].indirect(first_half(offsets)))
             nc.scalar.activation(tile[:, HALF:SLOTS], window[:].indirect(second_half(offsets)), COPY)
+            return tile
+
+        def combined(name, banks, other, op, share):
+            tile = keep.tile([P, COLS], F32, name=name)
+            staged = keep.tile([P, share], F32, name=name + "_staged")
+            nc.scalar.activation(staged[:], banks[0][:, 0:share], COPY)
+            nc.gpsimd.tensor_tensor(tile[:, 0:share], staged[:], other[:, 0:share], op)
+            nc.vector.tensor_tensor(tile[:, BANK:COLS], banks[1][:], other[:, BANK:COLS], op)
+            nc.vector.tensor_tensor(tile[:, share:BANK], banks[0][:, share:BANK], other[:, share:BANK], op)
             return tile
 
         q_raw = keep.tile([P, PACK, Q], F32, name="q_raw")
@@ -142,20 +153,14 @@ def tile_attend_tributaries_four_kernel(
         d0 = [scores("d_acc%d" % h, 2 + h, shelves_w, shelves_s, FP4X4, 2, h * BANK, BANK) for h in range(2)]
 
         m1 = keep.tile([P, COLS], F32, name="m1")
-        for h in range(2):
+        for h in (1, 0):
             cols = slice(h * BANK, (h + 1) * BANK)
             nc.vector.tensor_tensor(m1[:, cols], f1[:, cols], f2[:, cols], ALU.min)
-        cc = keep.tile([P, COLS], F32, name="cc")
-        for h in range(2):
-            cols = slice(h * BANK, (h + 1) * BANK)
-            nc.vector.tensor_tensor(cc[:, cols], c0[h][:], m1[:, cols], ALU.add)
+        cc = combined("cc", c0, m1, ALU.add, ADD_SHARE)
         cc_picked = picked("cc_picked", cc, idx5)
         nc.vector.tensor_copy(f3[:].indirect(idx6[:]), cc_picked[:])
 
-        dd = keep.tile([P, COLS], F32, name="dd")
-        for h in range(2):
-            cols = slice(h * BANK, (h + 1) * BANK)
-            nc.vector.tensor_tensor(dd[:, cols], d0[h][:], f3[:, cols], ALU.subtract)
+        dd = combined("dd", d0, f3, ALU.subtract, SUBTRACT_SHARE)
         y_first = keep.tile([P, HALF], F32, name="y_first")
         y_second = keep.tile([P, HALF], F32, name="y_second")
         nc.vector.tensor_copy(y_first[:], dd[:].indirect(first_half(idx7)))

@@ -88,8 +88,10 @@ def tile_attend_tributaries_four_kernel(
         notes_w = load_words("notes_w", notes_words[0], 2)
         idx2 = load_list("idx2", offs2)
         idx4 = load_list("idx4", offs4)
-        keys_w = load_words("keys_w", keys_words[0].rearrange("p n t -> p (n t)"), 4)
+        keys_bytes = keys_words[0].rearrange("p n t -> p (n t)")
+        keys_low = load_words("keys_low", keys_bytes[:, 0 : 4 * BANK], 2)
         keys_s = load_scales(scale_tile("keys_tile", nc.gpsimd), 0, keys_scales)
+        keys_high = load_words("keys_high", keys_bytes[:, 4 * BANK : 4 * COLS], 2)
         idx = load_list("idx", offs)
         idx3 = load_list("idx3", offs3)
         f2 = zeroed("f2", "f2")
@@ -115,13 +117,13 @@ def tile_attend_tributaries_four_kernel(
         )
         f3 = zeroed("f3", "late")
 
-        def scores(name, bank, words, plane, dtype, bytes_per_column, start, width):
+        def scores(name, bank, words, plane, dtype, bytes_per_column, start, width, first=0):
             acc = psum.tile([P, width], F32, name=name, tag="bank%d" % bank)
             nc.tensor.matmul_mx(
                 out=acc[:],
                 lhsT=q_codes[:].bitcast(FP8X4),
                 lhsT_scale=q_scales[:],
-                rhs=words[:, start * bytes_per_column : (start + width) * bytes_per_column].bitcast(dtype),
+                rhs=words[:, (start - first) * bytes_per_column : (start - first + width) * bytes_per_column].bitcast(dtype),
                 rhs_scale=plane[:, start : start + width],
                 start=True,
                 stop=True,
@@ -142,9 +144,11 @@ def tile_attend_tributaries_four_kernel(
         nc.vector.tensor_copy(f2[:].indirect(idx4[:]), b_picked[:])
 
         a = keep.tile([P, COLS], F32, name="a")
-        for piece in range(2):
-            acc = scores("a_acc%d" % piece, 5 + piece, keys_w, keys_s, FP8X4, 4, piece * BANK, BANK)
-            nc.scalar.activation(a[:, piece * BANK : (piece + 1) * BANK], acc[:], COPY)
+        for piece, (words, first, start, width) in enumerate(
+            ((keys_low, 0, 0, 512), (keys_high, 512, 512, 256), (keys_high, 512, 768, 256))
+        ):
+            acc = scores("a_acc%d" % piece, 5 + piece, words, keys_s, FP8X4, 4, start, width, first)
+            nc.scalar.activation(a[:, start : start + width], acc[:], COPY)
         a_picked = keep.tile([P, SLOTS], F32, name="a_picked")
         nc.scalar.activation(a_picked[:], a[:].indirect(idx[:]), COPY)
         nc.vector.tensor_copy(f1[:].indirect(idx3[:]), a_picked[:])

from contextlib import ExitStack

import concourse.mybir as mybir

D, COLS, SLOTS, Q = 512, 1024, 512, 128
FLOPS = 4 * 2 * D * Q * COLS

F32 = mybir.dt.float32
BF16 = mybir.dt.bfloat16
I32 = mybir.dt.int32
U32 = mybir.dt.uint32
U16 = mybir.dt.uint16
U8 = mybir.dt.uint8
FP8X4 = mybir.dt.float8_e4m3fn_x4
FP4X4 = mybir.dt.float4_e2m1fn_x4
ALU = mybir.AluOpType
COPY = mybir.ActivationFunctionType.Copy

P = 128
PACK = 4
BANK = 512
HALF = SLOTS // 2
LIST_COLS = SLOTS // 16
ADD_SHARE = 256
SUBTRACT_SHARE = 304


def tile_attend_tributaries_four_kernel(
    tc, query, keys_words, keys_scales, notes_words, notes_scales, users_words, users_scales,
    shelves_words, shelves_scales, offs, offs2, offs3, offs4, offs5, offs6, offs7, out,
):
    nc = tc.nc
    with ExitStack() as ctx:
        lists = ctx.enter_context(tc.tile_pool(name="lists", bufs=1))
        keep = ctx.enter_context(tc.tile_pool(name="keep", bufs=1))
        psum = ctx.enter_context(tc.psum_pool(name="psum", bufs=1))

        def load_list(name, source):
            tile = lists.tile([P, LIST_COLS], U16, name=name)
            nc.sync.dma_start(tile[:], source)
            return tile

        def scale_tile(name, engine):
            tile = keep.tile([P, COLS], U8, name=name, align_bytes=64)
            engine.memset(tile[:].bitcast(I32), 0)
            return tile

        def load_scales(tile, first_row, source):
            rows = source[0].bitcast(I32)
            for r in range(4):
                nc.sync.dma_start(tile[first_row + r : P : 32, :].bitcast(I32), rows[r:16:4, :])
            return tile[first_row:P, :]

        def load_words(name, source, bytes_per_column):
            words = keep.tile([P, COLS * bytes_per_column], U8, name=name, align_bytes=64)
            nc.sync.dma_start(words[:].bitcast(I32), source.bitcast(I32))
            return words

        def zeroed(name, tag):
            tile = keep.tile([P, COLS], F32, name=name, tag=tag, align_bytes=64)
            nc.vector.memset(tile[:].bitcast(I32), 0)
            return tile

        def first_half(tile):
            return tile[:, 0 : LIST_COLS // 2]

        def second_half(tile):
            return tile[:, LIST_COLS // 2 : LIST_COLS]

        def picked(name, window, offsets):
            tile = keep.tile([P, SLOTS], F32, name=name)
            nc.vector.tensor_copy(tile[:, 0:HALF], window[:].indirect(first_half(offsets)))
            nc.scalar.activation(tile[:, HALF:SLOTS], window[:].indirect(second_half(offsets)), COPY)
            return tile

        def combined(name, banks, other, op, share):
            tile = keep.tile([P, COLS], F32, name=name)
            staged = keep.tile([P, share], F32, name=name + "_staged")
            nc.scalar.activation(staged[:], banks[0][:, 0:share], COPY)
            nc.gpsimd.tensor_tensor(tile[:, 0:share], staged[:], other[:, 0:share], op)
            nc.vector.tensor_tensor(tile[:, BANK:COLS], banks[1][:], other[:, BANK:COLS], op)
            nc.vector.tensor_tensor(tile[:, share:BANK], banks[0][:, share:BANK], other[:, share:BANK], op)
            return tile

        q_raw = keep.tile([P, PACK, Q], F32, name="q_raw")
        nc.sync.dma_start(q_raw[:], query.rearrange("(p j) w -> p j w", j=PACK))
        notes_s = load_scales(scale_tile("notes_tile", nc.vector), 0, notes_scales)
        notes_w = load_words("notes_w", notes_words[0], 2)
        idx2 = load_list("idx2", offs2)
        idx4 = load_list("idx4", offs4)
        keys_bytes = keys_words[0].rearrange("p n t -> p (n t)")
        keys_low = load_words("keys_low", keys_bytes[:, 0 : 4 * BANK], 2)
        keys_s = load_scales(scale_tile("keys_tile", nc.gpsimd), 0, keys_scales)
        keys_high = load_words("keys_high", keys_bytes[:, 4 * BANK : 4 * COLS], 2)
        idx = load_list("idx", offs)
        idx3 = load_list("idx3", offs3)
        f2 = zeroed("f2", "f2")
        f1 = zeroed("f1", "f1")
        shared_tile = scale_tile("shared_tile", nc.gpsimd)
        users_s = load_scales(shared_tile, 4, users_scales)
        users_w = load_words("users_w", users_words[0].rearrange("p n t -> p (n t)"), 4)
        idx5 = load_list("idx5", offs5)
        idx6 = load_list("idx6", offs6)
        shelves_s = load_scales(shared_tile, 0, shelves_scales)
        shelves_w = load_words("shelves_w", shelves_words[0], 2)
        idx7 = load_list("idx7", offs7)

        q_grouped = keep.tile([P, Q, PACK], BF16, name="q_grouped", tag="late", align_bytes=64)
        q_in = q_raw[:].rearrange("p t (c i) -> p c t i", i=4)
        q_out = q_grouped[:].rearrange("p (c i) t -> p c t i", i=4)
        nc.vector.tensor_copy(q_out[:, 0:16], q_in[:, 0:16])
        nc.scalar.activation(q_out[:, 16:32], q_in[:, 16:32], COPY)
        q_codes = keep.tile([P, Q], U32, name="q_codes", align_bytes=64)
        q_scales = keep.tile([P, Q], U8, name="q_scales", align_bytes=64)
        nc.vector.quantize_mx(
            out=q_codes[:].bitcast(FP8X4), scales=q_scales[:], in_=q_grouped[:].rearrange("p w j -> p (w j)")
        )
        f3 = zeroed("f3", "late")

        def scores(name, bank, words, plane, dtype, bytes_per_column, start, width, first=0):
            acc = psum.tile([P, width], F32, name=name, tag="bank%d" % bank)
            nc.tensor.matmul_mx(
                out=acc[:],
                lhsT=q_codes[:].bitcast(FP8X4),
                lhsT_scale=q_scales[:],
                rhs=words[:, (start - first) * bytes_per_column : (start - first + width) * bytes_per_column].bitcast(dtype),
                rhs_scale=plane[:, start : start + width],
                start=True,
                stop=True,
            )
            return acc

        b = keep.tile([P, COLS], F32, name="b")
        start = 0
        for piece, width in enumerate((256, 256, 256, 128, 128)):
            acc = scores("b_acc%d" % piece, piece, notes_w, notes_s, FP4X4, 2, start, width)
            cols = slice(start, start + width)
            start = start + width
            if piece % 2 == 0:
                nc.scalar.activation(b[:, cols], acc[:], COPY)
            else:
                nc.vector.tensor_copy(b[:, cols], acc[:])
        b_picked = picked("b_picked", b, idx2)
        nc.vector.tensor_copy(f2[:].indirect(idx4[:]), b_picked[:])

        a = keep.tile([P, COLS], F32, name="a")
        for piece, (words, first, start, width) in enumerate(
            ((keys_low, 0, 0, 512), (keys_high, 512, 512, 256), (keys_high, 512, 768, 256))
        ):
            acc = scores("a_acc%d" % piece, 5 + piece, words, keys_s, FP8X4, 4, start, width, first)
            nc.scalar.activation(a[:, start : start + width], acc[:], COPY)
        a_picked = keep.tile([P, SLOTS], F32, name="a_picked")
        nc.scalar.activation(a_picked[:], a[:].indirect(idx[:]), COPY)
        nc.vector.tensor_copy(f1[:].indirect(idx3[:]), a_picked[:])

        c0 = [scores("c_acc%d" % h, h, users_w, users_s, FP8X4, 4, h * BANK, BANK) for h in range(2)]
        d0 = [scores("d_acc%d" % h, 2 + h, shelves_w, shelves_s, FP4X4, 2, h * BANK, BANK) for h in range(2)]

        m1 = keep.tile([P, COLS], F32, name="m1")
        for h in (1, 0):
            cols = slice(h * BANK, (h + 1) * BANK)
            nc.vector.tensor_tensor(m1[:, cols], f1[:, cols], f2[:, cols], ALU.min)
        cc = combined("cc", c0, m1, ALU.add, ADD_SHARE)
        cc_picked = picked("cc_picked", cc, idx5)
        nc.vector.tensor_copy(f3[:].indirect(idx6[:]), cc_picked[:])

        dd = combined("dd", d0, f3, ALU.subtract, SUBTRACT_SHARE)
        y_first = keep.tile([P, HALF], F32, name="y_first")
        y_second = keep.tile([P, HALF], F32, name="y_second")
        nc.vector.tensor_copy(y_first[:], dd[:].indirect(first_half(idx7)))
        nc.scalar.activation(y_second[:], dd[:].indirect(second_half(idx7)), COPY)
        nc.sync.dma_start(out[:, 0:HALF], y_first[:])
        nc.scalar.dma_start(out[:, HALF:SLOTS], y_second[:])
